import numpy as np, ml_dtypes
CORES = [97,101,225,229,353,357,481,485]
N = 8
NB, TK, FT = 4, 32, 4
def setup_inputs(rng):
    return {"x": rng.standard_normal((N, NB, 128, TK), dtype=np.float32).astype(ml_dtypes.bfloat16), "w1": (rng.standard_normal((N, 128, FT * 128), dtype=np.float32) / 8).astype(ml_dtypes.bfloat16), "w2": (rng.standard_normal((N, 128, FT * 128), dtype=np.float32) / np.float32(8 * np.sqrt(FT))).astype(ml_dtypes.bfloat16)}
def setup_inputs_big(rng):
    d = setup_inputs(rng)
    for k in ("x",): d[k] = (d[k].astype(np.float32) * 1048576.0).astype(d[k].dtype)
    return d
def setup_inputs_small(rng):
    d = setup_inputs(rng)
    for k in ("x",): d[k] = (d[k].astype(np.float32) * (1 / 1048576.0)).astype(d[k].dtype)
    return d
def reference(x, w1, w2):
    W1, W2 = w1.astype(np.float64), w2.astype(np.float64)
    a = x[0].astype(np.float64)
    for s in range(N):
        a = sum(np.einsum("kf,bkn->bfn", W2[s][:, 128 * f:128 * f + 128], np.maximum(np.einsum("kf,bkn->bfn", W1[s][:, 128 * f:128 * f + 128], a), 0.0)) for f in range(FT))
    y = np.full(x.shape, np.nan, ml_dtypes.bfloat16)
    y[N - 1] = a.astype(ml_dtypes.bfloat16)
    return {"y": y}

@@ -1,0 +1,122 @@
+from concourse.mybir import AluOpType
+
+P = 128
+FT = 4
+NB, TK = 4, 32
+COLS = NB * TK
+WID = FT * P
+SLOTS = 4
+
+SCRATCH = {
+    "w1s": ("sbuf", [P, SLOTS * WID], "bfloat16"),
+    "w2s": ("sbuf", [P, SLOTS * WID], "bfloat16"),
+    "acts": ("sbuf", [P, (SLOTS + 1) * COLS], "bfloat16"),
+    "hid": ("sbuf", [P, SLOTS * FT * COLS], "bfloat16"),
+    "zero": ("sbuf", [P, COLS], "float32"),
+    "p1_0": ("psum", [P, 512], "float32"),
+    "p1_1": ("psum", [P, 512], "float32"),
+    "p1_2": ("psum", [P, 512], "float32"),
+    "p1_3": ("psum", [P, 512], "float32"),
+    "p2": ("psum", [P, 512], "float32"),
+}
+SEMAPHORES = (["w1_%d" % j for j in range(SLOTS)] + ["w2_%d" % j for j in range(SLOTS)]
+              + ["ldx", "act", "sent", "pe", "ve", "zs", "st"])
+
+
+def _engines(mask, n):
+    bits = [b for b in range(16) if (mask >> b) & 1]
+    n = min(n, len(bits))
+    step = len(bits) // n
+    return sum(1 << b for b in bits[::step][:n]), n
+
+
+def rank_program(g, core, T, topo):
+    rank = T.rank_of(core)
+    if rank is None:
+        return
+    cores = T.cores
+    head, tail = cores[0], cores[-1]
+
+    def home_of(c):
+        return head if topo.rack(topo.host(c)) == topo.rack(topo.host(head)) else tail
+
+    home = home_of(core)
+    mine = [c for c in cores if home_of(c) == home]
+    slot = mine.index(core)
+    w1_own = T.w1s[:, slot * WID:(slot + 1) * WID]
+    w2_own = T.w2s[:, slot * WID:(slot + 1) * WID]
+    sem_w1 = [T.sem["w1_%d" % j] for j in range(SLOTS)]
+    sem_w2 = [T.sem["w2_%d" % j] for j in range(SLOTS)]
+
+    if core != home:
+        g.sync.dma_start(w1_own, T.w1[:, :]).then_inc(sem_w1[slot], 16)
+        g.sync.dma_start(w2_own, T.w2[:, :]).then_inc(sem_w2[slot], 16)
+        rid, pid = topo.addr(home, core)
+        m, n = _engines(topo.mask(core, home), 8)
+        g.wait_ge(sem_w1[slot], 16)
+        g.remote_dma(out_ap=w1_own, in_ap=w1_own, remote_sem=sem_w1[slot], local_sem=T.sem.sent,
+                     pid=pid, routing_id=rid, dma_engine_mask=m)
+        g.wait_ge(sem_w2[slot], 16)
+        g.remote_dma(out_ap=w2_own, in_ap=w2_own, remote_sem=sem_w2[slot], local_sem=T.sem.sent,
+                     pid=pid, routing_id=rid, dma_engine_mask=m)
+        g.wait_ge(T.sem.sent, 2 * n)
+        return
+
+    hop_mask, hop_n = _engines(topo.mask(head, tail), 8)
+    a_in = T.acts[:, 0:COLS]
+    if core == head:
+        for m_ in range(NB):
+            q = g.sync if m_ < NB // 2 else g.scalar
+            q.dma_start(T.acts[:, m_ * TK:(m_ + 1) * TK], T.x[m_]).then_inc(T.sem.ldx, 16)
+    g.sync.dma_start(w1_own, T.w1[:, :]).then_inc(sem_w1[slot], 16)
+    g.scalar.dma_start(w2_own, T.w2[:, :]).then_inc(sem_w2[slot], 16)
+
+    g.vector.memset(T.zero[:, :], 0.0).then_inc(T.sem.zs, 1)
+    g.vector.wait_ge(T.sem.zs, 1)
+
+    if core == head:
+        g.tensor.wait_ge(T.sem.ldx, 16 * NB)
+    else:
+        g.tensor.wait_ge(T.sem.act, hop_n)
+
+    p1 = [T["p1_%d" % f][:, 0:COLS] for f in range(FT)]
+    p2 = T.p2[:, 0:COLS]
+    pe, ve = 0, 0
+    for j, c in enumerate(mine):
+        arrived = 16 if c == core else _engines(topo.mask(c, core), 8)[1]
+        a = T.acts[:, j * COLS:(j + 1) * COLS]
+        a_out = T.acts[:, (j + 1) * COLS:(j + 2) * COLS]
+        h = [T.hid[:, (j * FT + f) * COLS:(j * FT + f + 1) * COLS] for f in range(FT)]
+        g.tensor.wait_ge(sem_w1[j], arrived)
+        if j > 0:
+            g.tensor.wait_ge(T.sem.ve, ve)
+        for f in range(FT):
+            g.tensor.matmul(p1[f], T.w1s[:, j * WID + f * P:j * WID + (f + 1) * P], a,
+                            start=True, stop=True).then_inc(T.sem.pe, 1)
+            pe += 1
+            g.vector.wait_ge(T.sem.pe, pe)
+            g.vector.tensor_tensor(h[f], p1[f], T.zero[:, :], AluOpType.max).then_inc(T.sem.ve, 1)
+        g.tensor.wait_ge(sem_w2[j], arrived)
+        for f in range(FT):
+            ve += 1
+            g.tensor.wait_ge(T.sem.ve, ve)
+            g.tensor.matmul(p2, T.w2s[:, j * WID + f * P:j * WID + (f + 1) * P], h[f],
+                            start=(f == 0), stop=(f == FT - 1)).then_inc(T.sem.pe, 1)
+            pe += 1
+        g.vector.wait_ge(T.sem.pe, pe)
+        g.vector.tensor_copy(a_out, p2).then_inc(T.sem.ve, 1)
+        ve += 1
+
+    last = T.acts[:, SLOTS * COLS:(SLOTS + 1) * COLS]
+    if core == head:
+        rid, pid = topo.addr(tail, head)
+        g.wait_ge(T.sem.ve, ve)
+        g.remote_dma(out_ap=a_in, in_ap=last, remote_sem=T.sem.act, local_sem=T.sem.sent,
+                     pid=pid, routing_id=rid, dma_engine_mask=hop_mask)
+        g.wait_ge(T.sem.sent, hop_n)
+    else:
+        for q, blocks in ((g.sync, range(0, NB // 2)), (g.scalar, range(NB // 2, NB))):
+            q.wait_ge(T.sem.ve, ve)
+            for m_ in blocks:
+                q.dma_start(T.y[m_], T.acts[:, SLOTS * COLS + m_ * TK:SLOTS * COLS + (m_ + 1) * TK]).then_inc(T.sem.st, 16)
+        g.wait_ge(T.sem.st, 16 * NB)

@@ -4,6 +4,8 @@ P = 128
 FT = 4
 NB, TK = 4, 32
 COLS = NB * TK
+NS = 2
+H = COLS // NS
 WID = FT * P
 SLOTS = 4
 
@@ -12,12 +14,15 @@ SCRATCH = {
     "w2s": ("sbuf", [P, SLOTS * WID], "bfloat16"),
     "acts": ("sbuf", [P, (SLOTS + 1) * COLS], "bfloat16"),
     "hid": ("sbuf", [P, SLOTS * FT * COLS], "bfloat16"),
-    "zero": ("sbuf", [P, COLS], "float32"),
-    "p1_0": ("psum", [P, 512], "float32"),
-    "p1_1": ("psum", [P, 512], "float32"),
-    "p1_2": ("psum", [P, 512], "float32"),
-    "p1_3": ("psum", [P, 512], "float32"),
-    "p2": ("psum", [P, 512], "float32"),
+    "zero": ("sbuf", [P, H], "float32"),
+    "pa_0": ("psum", [P, 512], "float32"),
+    "pa_1": ("psum", [P, 512], "float32"),
+    "pa_2": ("psum", [P, 512], "float32"),
+    "pa_3": ("psum", [P, 512], "float32"),
+    "pb_0": ("psum", [P, 512], "float32"),
+    "pb_1": ("psum", [P, 512], "float32"),
+    "p2_0": ("psum", [P, 512], "float32"),
+    "p2_1": ("psum", [P, 512], "float32"),
 }
 SEMAPHORES = (["w1_%d" % j for j in range(SLOTS)] + ["w2_%d" % j for j in range(SLOTS)]
               + ["ldx", "act", "sent", "pe", "ve", "zs", "st"])
@@ -79,33 +84,48 @@ def rank_program(g, core, T, topo):
     else:
         g.tensor.wait_ge(T.sem.act, hop_n)
 
-    p1 = [T["p1_%d" % f][:, 0:COLS] for f in range(FT)]
-    p2 = T.p2[:, 0:COLS]
+    p1 = [[T["pa_%d" % f][:, 0:H] for f in range(FT)],
+          [T["pb_%d" % (f // 2)][:, (f % 2) * H:(f % 2 + 1) * H] for f in range(FT)]]
+    p2 = [T["p2_%d" % k][:, 0:H] for k in range(NS)]
     pe, ve = 0, 0
+    copied = [0] * NS
     for j, c in enumerate(mine):
         arrived = 16 if c == core else _engines(topo.mask(c, core), 8)[1]
-        a = T.acts[:, j * COLS:(j + 1) * COLS]
-        a_out = T.acts[:, (j + 1) * COLS:(j + 2) * COLS]
-        h = [T.hid[:, (j * FT + f) * COLS:(j * FT + f + 1) * COLS] for f in range(FT)]
+        a = [T.acts[:, j * COLS + k * H:j * COLS + (k + 1) * H] for k in range(NS)]
+        a_out = [T.acts[:, (j + 1) * COLS + k * H:(j + 1) * COLS + (k + 1) * H] for k in range(NS)]
+        h = [[T.hid[:, (j * FT + f) * COLS + k * H:(j * FT + f) * COLS + (k + 1) * H] for f in range(FT)]
+             for k in range(NS)]
         g.tensor.wait_ge(sem_w1[j], arrived)
-        if j > 0:
-            g.tensor.wait_ge(T.sem.ve, ve)
-        for f in range(FT):
-            g.tensor.matmul(p1[f], T.w1s[:, j * WID + f * P:j * WID + (f + 1) * P], a,
-                            start=True, stop=True).then_inc(T.sem.pe, 1)
-            pe += 1
-            g.vector.wait_ge(T.sem.pe, pe)
-            g.vector.tensor_tensor(h[f], p1[f], T.zero[:, :], AluOpType.max).then_inc(T.sem.ve, 1)
+        made = {}
+        for k in range(NS):
+            if j > 0:
+                g.tensor.wait_ge(T.sem.ve, copied[k])
+            for f in range(FT):
+                g.tensor.matmul(p1[k][f], T.w1s[:, j * WID + f * P:j * WID + (f + 1) * P], a[k],
+                                start=True, stop=True).then_inc(T.sem.pe, 1)
+                pe += 1
+                made[k, f] = pe
+        maxed = {}
+        for k in range(NS):
+            for f in range(FT):
+                g.vector.wait_ge(T.sem.pe, made[k, f] if k == 0 else made[k, f | 1])
+                g.vector.tensor_tensor(h[k][f], p1[k][f], T.zero[:, :], AluOpType.max).then_inc(T.sem.ve, 1)
+                ve += 1
+                maxed[k, f] = ve
         g.tensor.wait_ge(sem_w2[j], arrived)
-        for f in range(FT):
+        summed = [0] * NS
+        for k in range(NS):
+            for f in range(FT):
+                g.tensor.wait_ge(T.sem.ve, maxed[k, f])
+                g.tensor.matmul(p2[k], T.w2s[:, j * WID + f * P:j * WID + (f + 1) * P], h[k][f],
+                                start=(f == 0), stop=(f == FT - 1)).then_inc(T.sem.pe, 1)
+                pe += 1
+            summed[k] = pe
+        for k in range(NS):
+            g.vector.wait_ge(T.sem.pe, summed[k])
+            g.vector.tensor_copy(a_out[k], p2[k]).then_inc(T.sem.ve, 1)
             ve += 1
-            g.tensor.wait_ge(T.sem.ve, ve)
-            g.tensor.matmul(p2, T.w2s[:, j * WID + f * P:j * WID + (f + 1) * P], h[f],
-                            start=(f == 0), stop=(f == FT - 1)).then_inc(T.sem.pe, 1)
-            pe += 1
-        g.vector.wait_ge(T.sem.pe, pe)
-        g.vector.tensor_copy(a_out, p2).then_inc(T.sem.ve, 1)
-        ve += 1
+            copied[k] = ve
 
     last = T.acts[:, SLOTS * COLS:(SLOTS + 1) * COLS]
     if core == head:

@@ -24,8 +24,9 @@ SCRATCH = {
     "p2_0": ("psum", [P, 512], "float32"),
     "p2_1": ("psum", [P, 512], "float32"),
 }
-SEMAPHORES = (["w1_%d" % j for j in range(SLOTS)] + ["w2_%d" % j for j in range(SLOTS)]
-              + ["ldx", "act", "sent", "pe", "ve", "zs", "st"])
+SEMAPHORES = (["w0_%d" % j for j in range(SLOTS)] + ["w1_%d" % j for j in range(SLOTS)]
+              + ["w2_%d" % j for j in range(SLOTS)] + ["act_%d" % k for k in range(NS)]
+              + ["ldx", "sent", "pe", "ve", "zs", "st"])
 
 
 def _engines(mask, n):
@@ -45,98 +46,187 @@ def rank_program(g, core, T, topo):
     def home_of(c):
         return head if topo.rack(topo.host(c)) == topo.rack(topo.host(head)) else tail
 
+    def place(c):
+        return topo.host(c), topo.chip(c)
+
+    def aide_of(hm):
+        return [c for c in cores if c != hm and place(c) == place(hm)][0]
+
     home = home_of(core)
+    aide = aide_of(home)
+    second, partner = aide_of(head), aide_of(tail)
     mine = [c for c in cores if home_of(c) == home]
     slot = mine.index(core)
-    w1_own = T.w1s[:, slot * WID:(slot + 1) * WID]
-    w2_own = T.w2s[:, slot * WID:(slot + 1) * WID]
+    far = [j for j, c in enumerate(mine) if c != home and c != aide]
+    sem_w0 = [T.sem["w0_%d" % j] for j in range(SLOTS)]
     sem_w1 = [T.sem["w1_%d" % j] for j in range(SLOTS)]
     sem_w2 = [T.sem["w2_%d" % j] for j in range(SLOTS)]
+    sem_act = [T.sem["act_%d" % k] for k in range(NS)]
+
+    def w_first(j):
+        return T.w1s[:, j * WID:j * WID + P]
+
+    def w_rest(j):
+        return T.w1s[:, j * WID + P:(j + 1) * WID]
+
+    def w_one(j):
+        return T.w1s[:, j * WID:(j + 1) * WID]
+
+    def w_two(j):
+        return T.w2s[:, j * WID:(j + 1) * WID]
+
+    def table(t, k):
+        return T.acts[:, t * COLS + k * H:t * COLS + (k + 1) * H]
+
+    left = [0]
+
+    def write(dst, out_ap, in_ap, sem, mask, n):
+        rid, pid = topo.addr(dst, core)
+        g.remote_dma(out_ap=out_ap, in_ap=in_ap, remote_sem=sem, local_sem=T.sem.sent,
+                     pid=pid, routing_id=rid, dma_engine_mask=mask)
+        left[0] += n
 
     if core != home:
-        g.sync.dma_start(w1_own, T.w1[:, :]).then_inc(sem_w1[slot], 16)
-        g.sync.dma_start(w2_own, T.w2[:, :]).then_inc(sem_w2[slot], 16)
-        rid, pid = topo.addr(home, core)
-        m, n = _engines(topo.mask(core, home), 8)
-        g.wait_ge(sem_w1[slot], 16)
-        g.remote_dma(out_ap=w1_own, in_ap=w1_own, remote_sem=sem_w1[slot], local_sem=T.sem.sent,
-                     pid=pid, routing_id=rid, dma_engine_mask=m)
-        g.wait_ge(sem_w2[slot], 16)
-        g.remote_dma(out_ap=w2_own, in_ap=w2_own, remote_sem=sem_w2[slot], local_sem=T.sem.sent,
-                     pid=pid, routing_id=rid, dma_engine_mask=m)
-        g.wait_ge(T.sem.sent, 2 * n)
-        return
+        g.sync.dma_start(w_first(slot), T.w1[:, 0:P]).then_inc(sem_w0[slot], 16)
+        g.scalar.dma_start(w_two(slot), T.w2[:, :]).then_inc(sem_w2[slot], 16)
+        g.sync.dma_start(w_rest(slot), T.w1[:, P:WID]).then_inc(sem_w1[slot], 16)
+        allowed = topo.mask(core, home)
+        if core == second:
+            allowed &= topo.mask(core, tail)
+        m_home, n_home = _engines(allowed, 8)
+        for piece, sem in ((w_first(slot), sem_w0[slot]), (w_rest(slot), sem_w1[slot]), (w_two(slot), sem_w2[slot])):
+            g.wait_ge(sem, 16)
+            write(home, piece, piece, sem, m_home, n_home)
+        if core != aide:
+            g.wait_ge(T.sem.sent, left[0])
+            return
 
-    hop_mask, hop_n = _engines(topo.mask(head, tail), 8)
-    a_in = T.acts[:, 0:COLS]
+    hop_mask, hop_n = _engines(topo.mask(head, partner) & topo.mask(head, second), 8)
+    fw_mask, fw_n = _engines(topo.mask(home, aide), 16)
+
+    def streams_of(j):
+        if core == head:
+            return [0, 1] if j < far[0] else [0]
+        if core == second:
+            return [] if j < far[0] else [1]
+        return [0] if core == partner else [1]
+
+    first = 1 if core in (second, tail) else 0
+
     if core == head:
         for m_ in range(NB):
             q = g.sync if m_ < NB // 2 else g.scalar
             q.dma_start(T.acts[:, m_ * TK:(m_ + 1) * TK], T.x[m_]).then_inc(T.sem.ldx, 16)
-    g.sync.dma_start(w1_own, T.w1[:, :]).then_inc(sem_w1[slot], 16)
-    g.scalar.dma_start(w2_own, T.w2[:, :]).then_inc(sem_w2[slot], 16)
+    if core == home:
+        g.sync.dma_start(w_one(slot), T.w1[:, :]).then_inc(sem_w1[slot], 16)
+        g.scalar.dma_start(w_two(slot), T.w2[:, :]).then_inc(sem_w2[slot], 16)
 
     g.vector.memset(T.zero[:, :], 0.0).then_inc(T.sem.zs, 1)
     g.vector.wait_ge(T.sem.zs, 1)
 
-    if core == head:
-        g.tensor.wait_ge(T.sem.ldx, 16 * NB)
-    else:
-        g.tensor.wait_ge(T.sem.act, hop_n)
+    def landed(j, c):
+        if c == core:
+            if core == aide:
+                return (sem_w0[j], 16), (sem_w1[j], 16), (sem_w2[j], 16)
+            return (sem_w1[j], 16), None, (sem_w2[j], 16)
+        if core == aide:
+            if c == home:
+                return (sem_w1[j], fw_n), None, (sem_w2[j], fw_n)
+            return (sem_w0[j], fw_n), (sem_w1[j], fw_n), (sem_w2[j], fw_n)
+        n = _engines(topo.mask(c, core), 8)[1]
+        return (sem_w0[j], n), (sem_w1[j], n), (sem_w2[j], n)
 
-    p1 = [[T["pa_%d" % f][:, 0:H] for f in range(FT)],
-          [T["pb_%d" % (f // 2)][:, (f % 2) * H:(f % 2 + 1) * H] for f in range(FT)]]
+    def pass_on(j, part):
+        sem, n = landed(j, mine[j])[part]
+        ap = (w_first, w_rest, w_two)[part](j)
+        g.wait_ge(sem, n)
+        write(aide, ap, ap, sem, fw_mask, fw_n)
+
+    if core == tail:
+        for part in range(3):
+            for j in far:
+                pass_on(j, part)
+        for sem, ap in ((sem_w1[slot], w_one(slot)), (sem_w2[slot], w_two(slot))):
+            g.wait_ge(sem, 16)
+            write(aide, ap, ap, sem, fw_mask, fw_n)
+    if core == head:
+        pass_on(far[0], 0)
+        pass_on(far[0], 1)
+        g.tensor.wait_ge(T.sem.ldx, 16 * NB)
+
+    p1 = {}
+    for k in range(NS):
+        p1[k] = ([T["pa_%d" % f][:, 0:H] for f in range(FT)] if k == first else
+                 [T["pb_%d" % (f // 2)][:, (f % 2) * H:(f % 2 + 1) * H] for f in range(FT)])
     p2 = [T["p2_%d" % k][:, 0:H] for k in range(NS)]
     pe, ve = 0, 0
     copied = [0] * NS
     for j, c in enumerate(mine):
-        arrived = 16 if c == core else _engines(topo.mask(c, core), 8)[1]
-        a = [T.acts[:, j * COLS + k * H:j * COLS + (k + 1) * H] for k in range(NS)]
-        a_out = [T.acts[:, (j + 1) * COLS + k * H:(j + 1) * COLS + (k + 1) * H] for k in range(NS)]
+        streams = streams_of(j)
+        if not streams:
+            continue
+        s_first, s_rest, s_two = landed(j, c)
         h = [[T.hid[:, (j * FT + f) * COLS + k * H:(j * FT + f) * COLS + (k + 1) * H] for f in range(FT)]
              for k in range(NS)]
-        g.tensor.wait_ge(sem_w1[j], arrived)
-        made = {}
-        for k in range(NS):
-            if j > 0:
-                g.tensor.wait_ge(T.sem.ve, copied[k])
-            for f in range(FT):
-                g.tensor.matmul(p1[k][f], T.w1s[:, j * WID + f * P:j * WID + (f + 1) * P], a[k],
+        tseq = [(s, k, f) for s in (1, 2) for k in streams for f in range(FT)]
+        vseq = [(3, k, f) for k in streams for f in range(FT)] + [(4, k, 0) for k in streams]
+        pe_at = {op: pe + i + 1 for i, op in enumerate(tseq)}
+        ve_at = {op: ve + i + 1 for i, op in enumerate(vseq)}
+        pe += len(tseq)
+        ve += len(vseq)
+        two_there = False
+        for s, k, f in tseq:
+            if s == 1:
+                if f == 0:
+                    if copied[k]:
+                        g.tensor.wait_ge(T.sem.ve, copied[k])
+                    elif core != head:
+                        g.tensor.wait_ge(sem_act[k], hop_n)
+                if k == streams[0] and f == 0:
+                    g.tensor.wait_ge(s_first[0], s_first[1])
+                if k == streams[0] and f == 1 and s_rest is not None:
+                    g.tensor.wait_ge(s_rest[0], s_rest[1])
+                g.tensor.matmul(p1[k][f], T.w1s[:, j * WID + f * P:j * WID + (f + 1) * P], table(j, k),
                                 start=True, stop=True).then_inc(T.sem.pe, 1)
-                pe += 1
-                made[k, f] = pe
-        maxed = {}
-        for k in range(NS):
-            for f in range(FT):
-                g.vector.wait_ge(T.sem.pe, made[k, f] if k == 0 else made[k, f | 1])
-                g.vector.tensor_tensor(h[k][f], p1[k][f], T.zero[:, :], AluOpType.max).then_inc(T.sem.ve, 1)
-                ve += 1
-                maxed[k, f] = ve
-        g.tensor.wait_ge(sem_w2[j], arrived)
-        summed = [0] * NS
-        for k in range(NS):
-            for f in range(FT):
-                g.tensor.wait_ge(T.sem.ve, maxed[k, f])
+            else:
+                if not two_there:
+                    g.tensor.wait_ge(s_two[0], s_two[1])
+                    two_there = True
+                g.tensor.wait_ge(T.sem.ve, ve_at[3, k, f])
                 g.tensor.matmul(p2[k], T.w2s[:, j * WID + f * P:j * WID + (f + 1) * P], h[k][f],
                                 start=(f == 0), stop=(f == FT - 1)).then_inc(T.sem.pe, 1)
-                pe += 1
-            summed[k] = pe
-        for k in range(NS):
-            g.vector.wait_ge(T.sem.pe, summed[k])
-            g.vector.tensor_copy(a_out[k], p2[k]).then_inc(T.sem.ve, 1)
-            ve += 1
-            copied[k] = ve
+        for s, k, f in vseq:
+            if s == 3:
+                g.vector.wait_ge(T.sem.pe, pe_at[1, k, f if k == first else f | 1])
+                g.vector.tensor_tensor(h[k][f], p1[k][f], T.zero[:, :], AluOpType.max).then_inc(T.sem.ve, 1)
+            else:
+                g.vector.wait_ge(T.sem.pe, pe_at[2, k, FT - 1])
+                g.vector.tensor_copy(table(j + 1, k), p2[k]).then_inc(T.sem.ve, 1)
+                copied[k] = ve_at[s, k, f]
+        if core == head and j + 1 == far[0]:
+            g.wait_ge(T.sem.ve, copied[1])
+            write(aide, table(j + 1, 1), table(j + 1, 1), sem_act[1], hop_mask, hop_n)
+            pass_on(far[0], 2)
+            for jj in far[1:]:
+                for part in range(3):
+                    pass_on(jj, part)
 
-    last = T.acts[:, SLOTS * COLS:(SLOTS + 1) * COLS]
+    per = NB // NS
     if core == head:
-        rid, pid = topo.addr(tail, head)
-        g.wait_ge(T.sem.ve, ve)
-        g.remote_dma(out_ap=a_in, in_ap=last, remote_sem=T.sem.act, local_sem=T.sem.sent,
-                     pid=pid, routing_id=rid, dma_engine_mask=hop_mask)
-        g.wait_ge(T.sem.sent, hop_n)
+        g.wait_ge(T.sem.ve, copied[0])
+        write(partner, table(0, 0), table(SLOTS, 0), sem_act[0], hop_mask, hop_n)
+    elif core == second:
+        g.wait_ge(T.sem.ve, copied[1])
+        write(tail, table(0, 1), table(SLOTS, 1), sem_act[1], m_home, n_home)
+    elif core == partner:
+        g.wait_ge(T.sem.ve, copied[0])
+        write(tail, table(SLOTS, 0), table(SLOTS, 0), sem_act[0], m_home, n_home)
     else:
-        for q, blocks in ((g.sync, range(0, NB // 2)), (g.scalar, range(NB // 2, NB))):
-            q.wait_ge(T.sem.ve, ve)
-            for m_ in blocks:
+        n_in = _engines(topo.mask(partner, tail), 8)[1]
+        g.scalar.wait_ge(T.sem.ve, copied[1])
+        g.sync.wait_ge(sem_act[0], n_in)
+        for q, k in ((g.scalar, 1), (g.sync, 0)):
+            for m_ in range(k * per, (k + 1) * per):
                 q.dma_start(T.y[m_], T.acts[:, SLOTS * COLS + m_ * TK:SLOTS * COLS + (m_ + 1) * TK]).then_inc(T.sem.st, 16)
         g.wait_ge(T.sem.st, 16 * NB)
+    g.wait_ge(T.sem.sent, left[0])

from concourse.mybir import AluOpType

P = 128
FT = 4
NB, TK = 4, 32
COLS = NB * TK
NS = 2
H = COLS // NS
WID = FT * P
SLOTS = 4

SCRATCH = {
    "w1s": ("sbuf", [P, SLOTS * WID], "bfloat16"),
    "w2s": ("sbuf", [P, SLOTS * WID], "bfloat16"),
    "acts": ("sbuf", [P, (SLOTS + 1) * COLS], "bfloat16"),
    "hid": ("sbuf", [P, SLOTS * FT * COLS], "bfloat16"),
    "zero": ("sbuf", [P, H], "float32"),
    "pa_0": ("psum", [P, 512], "float32"),
    "pa_1": ("psum", [P, 512], "float32"),
    "pa_2": ("psum", [P, 512], "float32"),
    "pa_3": ("psum", [P, 512], "float32"),
    "pb_0": ("psum", [P, 512], "float32"),
    "pb_1": ("psum", [P, 512], "float32"),
    "p2_0": ("psum", [P, 512], "float32"),
    "p2_1": ("psum", [P, 512], "float32"),
}
SEMAPHORES = (["w0_%d" % j for j in range(SLOTS)] + ["w1_%d" % j for j in range(SLOTS)]
              + ["w2_%d" % j for j in range(SLOTS)] + ["act_%d" % k for k in range(NS)]
              + ["ldx", "sent", "pe", "ve", "zs", "st"])


def _engines(mask, n):
    bits = [b for b in range(16) if (mask >> b) & 1]
    n = min(n, len(bits))
    step = len(bits) // n
    return sum(1 << b for b in bits[::step][:n]), n


def rank_program(g, core, T, topo):
    rank = T.rank_of(core)
    if rank is None:
        return
    cores = T.cores
    head, tail = cores[0], cores[-1]

    def home_of(c):
        return head if topo.rack(topo.host(c)) == topo.rack(topo.host(head)) else tail

    def place(c):
        return topo.host(c), topo.chip(c)

    def aide_of(hm):
        return [c for c in cores if c != hm and place(c) == place(hm)][0]

    home = home_of(core)
    aide = aide_of(home)
    second, partner = aide_of(head), aide_of(tail)
    mine = [c for c in cores if home_of(c) == home]
    slot = mine.index(core)
    far = [j for j, c in enumerate(mine) if c != home and c != aide]
    sem_w0 = [T.sem["w0_%d" % j] for j in range(SLOTS)]
    sem_w1 = [T.sem["w1_%d" % j] for j in range(SLOTS)]
    sem_w2 = [T.sem["w2_%d" % j] for j in range(SLOTS)]
    sem_act = [T.sem["act_%d" % k] for k in range(NS)]

    def w_first(j):
        return T.w1s[:, j * WID:j * WID + P]

    def w_rest(j):
        return T.w1s[:, j * WID + P:(j + 1) * WID]

    def w_one(j):
        return T.w1s[:, j * WID:(j + 1) * WID]

    def w_two(j):
        return T.w2s[:, j * WID:(j + 1) * WID]

    def table(t, k):
        return T.acts[:, t * COLS + k * H:t * COLS + (k + 1) * H]

    left = [0]

    def write(dst, out_ap, in_ap, sem, mask, n):
        rid, pid = topo.addr(dst, core)
        g.remote_dma(out_ap=out_ap, in_ap=in_ap, remote_sem=sem, local_sem=T.sem.sent,
                     pid=pid, routing_id=rid, dma_engine_mask=mask)
        left[0] += n

    if core != home:
        g.sync.dma_start(w_first(slot), T.w1[:, 0:P]).then_inc(sem_w0[slot], 16)
        g.scalar.dma_start(w_two(slot), T.w2[:, :]).then_inc(sem_w2[slot], 16)
        g.sync.dma_start(w_rest(slot), T.w1[:, P:WID]).then_inc(sem_w1[slot], 16)
        allowed = topo.mask(core, home)
        if core == second:
            allowed &= topo.mask(core, tail)
        m_home, n_home = _engines(allowed, 8)
        for piece, sem in ((w_first(slot), sem_w0[slot]), (w_rest(slot), sem_w1[slot]), (w_two(slot), sem_w2[slot])):
            g.wait_ge(sem, 16)
            write(home, piece, piece, sem, m_home, n_home)
        if core != aide:
            g.wait_ge(T.sem.sent, left[0])
            return

    hop_mask, hop_n = _engines(topo.mask(head, partner) & topo.mask(head, second), 8)
    fw_mask, fw_n = _engines(topo.mask(home, aide), 16)

    def streams_of(j):
        if core == head:
            return [0, 1] if j < far[0] else [0]
        if core == second:
            return [] if j < far[0] else [1]
        return [0] if core == partner else [1]

    first = 1 if core in (second, tail) else 0

    if core == head:
        for m_ in range(NB):
            q = g.sync if m_ < NB // 2 else g.scalar
            q.dma_start(T.acts[:, m_ * TK:(m_ + 1) * TK], T.x[m_]).then_inc(T.sem.ldx, 16)
    if core == home:
        g.sync.dma_start(w_one(slot), T.w1[:, :]).then_inc(sem_w1[slot], 16)
        g.scalar.dma_start(w_two(slot), T.w2[:, :]).then_inc(sem_w2[slot], 16)

    g.vector.memset(T.zero[:, :], 0.0).then_inc(T.sem.zs, 1)
    g.vector.wait_ge(T.sem.zs, 1)

    def landed(j, c):
        if c == core:
            if core == aide:
                return (sem_w0[j], 16), (sem_w1[j], 16), (sem_w2[j], 16)
            return (sem_w1[j], 16), None, (sem_w2[j], 16)
        if core == aide:
            if c == home:
                return (sem_w1[j], fw_n), None, (sem_w2[j], fw_n)
            return (sem_w0[j], fw_n), (sem_w1[j], fw_n), (sem_w2[j], fw_n)
        n = _engines(topo.mask(c, core), 8)[1]
        return (sem_w0[j], n), (sem_w1[j], n), (sem_w2[j], n)

    def pass_on(j, part):
        sem, n = landed(j, mine[j])[part]
        ap = (w_first, w_rest, w_two)[part](j)
        g.wait_ge(sem, n)
        write(aide, ap, ap, sem, fw_mask, fw_n)

    if core == tail:
        for part in range(3):
            for j in far:
                pass_on(j, part)
        for sem, ap in ((sem_w1[slot], w_one(slot)), (sem_w2[slot], w_two(slot))):
            g.wait_ge(sem, 16)
            write(aide, ap, ap, sem, fw_mask, fw_n)
    if core == head:
        pass_on(far[0], 0)
        pass_on(far[0], 1)
        g.tensor.wait_ge(T.sem.ldx, 16 * NB)

    p1 = {}
    for k in range(NS):
        p1[k] = ([T["pa_%d" % f][:, 0:H] for f in range(FT)] if k == first else
                 [T["pb_%d" % (f // 2)][:, (f % 2) * H:(f % 2 + 1) * H] for f in range(FT)])
    p2 = [T["p2_%d" % k][:, 0:H] for k in range(NS)]
    pe, ve = 0, 0
    copied = [0] * NS
    for j, c in enumerate(mine):
        streams = streams_of(j)
        if not streams:
            continue
        s_first, s_rest, s_two = landed(j, c)
        h = [[T.hid[:, (j * FT + f) * COLS + k * H:(j * FT + f) * COLS + (k + 1) * H] for f in range(FT)]
             for k in range(NS)]
        tseq = [(s, k, f) for s in (1, 2) for k in streams for f in range(FT)]
        vseq = [(3, k, f) for k in streams for f in range(FT)] + [(4, k, 0) for k in streams]
        pe_at = {op: pe + i + 1 for i, op in enumerate(tseq)}
        ve_at = {op: ve + i + 1 for i, op in enumerate(vseq)}
        pe += len(tseq)
        ve += len(vseq)
        two_there = False
        for s, k, f in tseq:
            if s == 1:
                if f == 0:
                    if copied[k]:
                        g.tensor.wait_ge(T.sem.ve, copied[k])
                    elif core != head:
                        g.tensor.wait_ge(sem_act[k], hop_n)
                if k == streams[0] and f == 0:
                    g.tensor.wait_ge(s_first[0], s_first[1])
                if k == streams[0] and f == 1 and s_rest is not None:
                    g.tensor.wait_ge(s_rest[0], s_rest[1])
                g.tensor.matmul(p1[k][f], T.w1s[:, j * WID + f * P:j * WID + (f + 1) * P], table(j, k),
                                start=True, stop=True).then_inc(T.sem.pe, 1)
            else:
                if not two_there:
                    g.tensor.wait_ge(s_two[0], s_two[1])
                    two_there = True
                g.tensor.wait_ge(T.sem.ve, ve_at[3, k, f])
                g.tensor.matmul(p2[k], T.w2s[:, j * WID + f * P:j * WID + (f + 1) * P], h[k][f],
                                start=(f == 0), stop=(f == FT - 1)).then_inc(T.sem.pe, 1)
        for s, k, f in vseq:
            if s == 3:
                g.vector.wait_ge(T.sem.pe, pe_at[1, k, f if k == first else f | 1])
                g.vector.tensor_tensor(h[k][f], p1[k][f], T.zero[:, :], AluOpType.max).then_inc(T.sem.ve, 1)
            else:
                g.vector.wait_ge(T.sem.pe, pe_at[2, k, FT - 1])
                g.vector.tensor_copy(table(j + 1, k), p2[k]).then_inc(T.sem.ve, 1)
                copied[k] = ve_at[s, k, f]
        if core == head and j + 1 == far[0]:
            g.wait_ge(T.sem.ve, copied[1])
            write(aide, table(j + 1, 1), table(j + 1, 1), sem_act[1], hop_mask, hop_n)
            pass_on(far[0], 2)
            for jj in far[1:]:
                for part in range(3):
                    pass_on(jj, part)

    per = NB // NS
    if core == head:
        g.wait_ge(T.sem.ve, copied[0])
        write(partner, table(0, 0), table(SLOTS, 0), sem_act[0], hop_mask, hop_n)
    elif core == second:
        g.wait_ge(T.sem.ve, copied[1])
        write(tail, table(0, 1), table(SLOTS, 1), sem_act[1], m_home, n_home)
    elif core == partner:
        g.wait_ge(T.sem.ve, copied[0])
        write(tail, table(SLOTS, 0), table(SLOTS, 0), sem_act[0], m_home, n_home)
    else:
        n_in = _engines(topo.mask(partner, tail), 8)[1]
        g.scalar.wait_ge(T.sem.ve, copied[1])
        g.sync.wait_ge(sem_act[0], n_in)
        for q, k in ((g.scalar, 1), (g.sync, 0)):
            for m_ in range(k * per, (k + 1) * per):
                q.dma_start(T.y[m_], T.acts[:, SLOTS * COLS + m_ * TK:SLOTS * COLS + (m_ + 1) * TK]).then_inc(T.sem.st, 16)
        g.wait_ge(T.sem.st, 16 * NB)
    g.wait_ge(T.sem.sent, left[0])
